import numpy as np
import ml_dtypes


def mxq(x, axis, fmt="e4m3"):
    dtype, down = {"e4m3": (ml_dtypes.float8_e4m3fn, 7), "e5m2": (ml_dtypes.float8_e5m2, 14)}[fmt]
    v = np.moveaxis(np.asarray(x, np.float32).astype(ml_dtypes.bfloat16).astype(np.float64), axis, -1)
    blocks = v.reshape(v.shape[:-1] + (-1, 32))
    amax = np.abs(blocks).max(-1, keepdims=True)
    byte = np.maximum(np.where(amax > 0, np.frexp(amax)[1] - 1 + 127, 0) - down, 1)
    scale = np.exp2(byte - 127.0)
    codes = (blocks / scale).astype(np.float32).astype(dtype).astype(np.float64)
    return np.moveaxis((codes * scale).reshape(v.shape), -1, axis)


WIDE = False


def mx_kscale(k):
    if not WIDE:
        return np.ones(k)
    levels = np.array([10, -10, 5, -5, 0])
    if k % 512:
        return np.exp2(np.random.permutation(np.resize(levels, k // 32))).repeat(32)
    a = np.empty((k // 512, 16))
    for p in range(k // 512):
        a[p, :8] = np.random.permutation(np.resize(levels, 8))
        for g in range(8):
            far = levels[np.abs(levels - a[p, g]) >= 10]
            a[p, g + 8] = far[np.random.randint(len(far))]
    return np.exp2(a.ravel()).repeat(32)


def f64(x):
    return np.asarray(x).astype(np.float64)


def striped8(idx):
    return np.asarray(idx).reshape(8, -1, 16).transpose(0, 2, 1).reshape(128, -1).astype(np.uint16)


def unstriped8(offs):
    return offs.reshape(8, 16, -1).transpose(0, 2, 1).reshape(8, -1).astype(np.int64)


def pick8(x, idx, run):
    r = np.arange(len(x))
    return x[r[:, None], idx[r % (8 * run) // run]]


E2M1 = np.array([0.0, 0.5, 1.0, 1.5, 2.0, 3.0, 4.0, 6.0, -0.0, -0.5, -1.0, -1.5, -2.0, -3.0, -4.0, -6.0])


def pack_weight(w, fmt):
    k, n = w.shape
    w = f64(np.asarray(w, np.float32).astype(ml_dtypes.bfloat16)).reshape(k // 32, 32, n)
    amax = np.abs(w).max(1)
    if fmt == "e4m3":
        byte = np.frexp(amax)[1] - 1 + 127 - 7
    else:
        mant, ex = np.frexp(amax / 6.0)
        byte = np.where(mant > 0.5, ex, ex - 1) + 127
    byte = np.clip(np.where(amax > 0, byte, 1), 1, 254)
    scaled = (w * np.exp2(127.0 - byte)[:, None, :]).reshape(k, n).astype(np.float32)
    by_word = np.ascontiguousarray(scaled.reshape(k // 512, 128, 4, n).transpose(0, 1, 3, 2))
    if fmt == "e4m3":
        words = by_word.astype(ml_dtypes.float8_e4m3fn).view(np.uint8)
    else:
        c = by_word.astype(ml_dtypes.float4_e2m1fn).view(np.uint8) & 0xF
        words = (c[..., 0::2] | (c[..., 1::2] << 4)).reshape(k // 512, 128, 2 * n)
    return np.ascontiguousarray(words), np.ascontiguousarray(byte.astype(np.uint8).reshape(k // 512, 16, n))


def unpack_weight(words, scales, fmt):
    g, _, n = scales.shape
    words = np.ascontiguousarray(words).reshape(g, 128, n, -1)
    if fmt == "e4m3":
        vals = words.view(ml_dtypes.float8_e4m3fn).astype(np.float64)
    else:
        nib = np.empty((g, 128, n, 4), np.uint8)
        nib[..., 0::2] = words & 0xF
        nib[..., 1::2] = words >> 4
        vals = E2M1[nib]
    vals = vals * np.repeat(np.exp2(scales.astype(np.float64) - 127.0), 8, axis=1)[..., None]
    return vals.transpose(0, 1, 3, 2).reshape(g * 512, n)


D, E, T, Q, I = 512, 512, 1024, 128, 512


def setup_inputs():
    n = np.random.standard_normal
    idx = np.stack([np.random.permutation(T)[:I] for _ in range(8)])
    idx2 = np.stack([np.random.permutation(T)[:I] for _ in range(8)])
    fd = mx_kscale(D)
    fe = mx_kscale(E)
    keysp = pack_weight(n((D, T)) / fd[:, None], "e4m3")
    return {
        "query": (n((D, Q)) * 0.6 / np.sqrt(D) * fd[:, None]).astype(np.float32),
        "keys_words": keysp[0],
        "keys_scales": keysp[1],
        "gout": (n((E, Q)) * 1 / np.sqrt(E) * fe[:, None]).astype(np.float32),
        "vals": (n((E, T)) / fe[:, None]).astype(np.float32),
        "share": (np.random.uniform(0.2, 0.9, (1, I))).astype(np.float32),
        "fac": (np.random.uniform(0.5, 2.0, (1, T))).astype(np.float32),
        "old": (0.5 * n((Q, T))).astype(np.float32),
        "offs": striped8(idx),
        "offs2": striped8(idx2),
    }


def reference(query, keys_words, keys_scales, gout, vals, share, fac, old, offs, offs2):
    idx = unstriped8(offs)
    idx2 = unstriped8(offs2)
    keysu = unpack_weight(keys_words, keys_scales, "e4m3")
    queryq = mxq(f64(query), 0, "e4m3")
    a = queryq.T @ keysu
    p = np.exp(a)
    z = np.sum(p, axis=1, keepdims=True)
    r = np.exp(pick8(a, idx, 16))
    ra = r * f64(share)
    rf = np.zeros((Q, T))
    rf[np.arange(Q)[:, None], idx[np.arange(Q) % 128 // 16]] = r
    rg = np.zeros((Q, T))
    rg[np.arange(Q)[:, None], idx2[np.arange(Q) % 128 // 16]] = ra
    goutq = mxq(f64(gout), 0, "e4m3")
    valsq = mxq(f64(vals), 0, "e4m3")
    c0 = goutq.T @ valsq
    drg = c0 / z * f64(fac)
    drf = c0 / z * f64(fac) * (-1.0)
    dra = pick8(drg, idx2, 16)
    dr = pick8(drf, idx, 16) + dra * f64(share)
    dz = np.sum(c0 * (p - rf + rg) * f64(fac) / np.square(z) * (-1.0), axis=1, keepdims=True)
    dp = c0 / z * f64(fac) + dz
    e1 = dr * r
    s1 = np.zeros((Q, T))
    s1[np.arange(Q)[:, None], idx[np.arange(Q) % 128 // 16]] = e1
    da = dp * p + s1
    y = da * 1024.0 + f64(old)
    return y

@@ -1,0 +1,217 @@
+from contextlib import ExitStack
+
+import concourse.mybir as mybir
+from concourse.masks import make_identity
+
+F32 = mybir.dt.float32
+BF16 = mybir.dt.bfloat16
+I32 = mybir.dt.int32
+U32 = mybir.dt.uint32
+U16 = mybir.dt.uint16
+U8 = mybir.dt.uint8
+FP8X4 = mybir.dt.float8_e4m3fn_x4
+ALU = mybir.AluOpType
+ACT = mybir.ActivationFunctionType
+AX = mybir.AxisListType
+
+P = 128
+PACK = 4
+T = 1024
+SLOTS = 512
+BANK = 512
+CHUNK = 256
+GAIN = 1024.0
+
+FLOPS = 2 * 2 * 512 * 128 * 1024
+
+
+def tile_attend_bpassedon_heads_kernel(tc, query, keys_words, keys_scales, gout, vals, share, fac, old, offs, offs2, out):
+    nc = tc.nc
+    halves = [slice(h * BANK, (h + 1) * BANK) for h in range(T // BANK)]
+
+    with ExitStack() as ctx:
+        sb = ctx.enter_context(tc.tile_pool(name="sb", bufs=1))
+        ps = ctx.enter_context(tc.psum_pool(name="ps", bufs=1))
+
+        def bank(tag):
+            return ps.tile([P, BANK], F32, name=tag, tag=tag)
+
+        def interleave(copy, grouped, raw):
+            copy(out=grouped[:].rearrange("p (c i) t -> p c t i", i=4), in_=raw[:].rearrange("p t (c i) -> p c t i", i=4))
+
+        def quantize(name, grouped, width):
+            codes = sb.tile([P, width], U32, name=name + "_codes", align_bytes=64)
+            scales = sb.tile([P, width], U8, name=name + "_scales", align_bytes=64)
+            nc.vector.quantize_mx(out=codes[:].bitcast(FP8X4), scales=scales[:], in_=grouped[:].rearrange("p w t -> p (w t)"))
+            return codes, scales
+
+        def turn(dst, src, first, last):
+            for j in range(BANK // P):
+                cols = slice(j * P, (j + 1) * P)
+                nc.tensor.matmul(dst[:, cols], lhsT=src[:, cols], rhs=ident[:], is_transpose=True,
+                                 start=(first and j == 0), stop=(last and j == BANK // P - 1))
+
+        k_scales = sb.tile([P, T], U8, align_bytes=64)
+        nc.vector.memset(k_scales[:].bitcast(I32), 0)
+        q_raw = sb.tile([P, PACK, P], F32)
+        nc.sync.dma_start(out=q_raw[:], in_=query.rearrange("(p j) w -> p j w", j=PACK))
+        for quad in range(4):
+            nc.scalar.dma_start(out=k_scales[32 * quad : 32 * quad + 4, :].bitcast(I32),
+                                in_=keys_scales[0, 4 * quad : 4 * quad + 4, :].bitcast(I32))
+        k_words = keys_words[0].rearrange("p n t -> p (n t)").bitcast(I32)
+        k_codes = []
+        for h, cols in enumerate(halves):
+            codes = sb.tile([P, BANK], U32, name=f"k_codes{h}", align_bytes=64)
+            nc.sync.dma_start(out=codes[:].bitcast(I32), in_=k_words[:, cols])
+            k_codes.append(codes)
+        fac_cols = sb.tile([P, T // BANK, PACK], F32)
+        nc.sync.dma_start(out=fac_cols[:], in_=fac[0].rearrange("(h p j) -> p h j", p=P, j=PACK))
+        share_cols = sb.tile([P, PACK], F32)
+        nc.sync.dma_start(out=share_cols[:], in_=share[0].rearrange("(p j) -> p j", j=PACK))
+        list1 = sb.tile([P, SLOTS // 16], U16)
+        nc.sync.dma_start(list1[:], offs)
+        g_raw = sb.tile([P, PACK, P], F32)
+        nc.sync.dma_start(out=g_raw[:], in_=gout.rearrange("(p j) w -> p j w", j=PACK))
+        v_rows = vals.rearrange("(p j) w -> p j w", j=PACK)
+        v_raw = []
+        for c in range(T // CHUNK):
+            raw = sb.tile([P, PACK, CHUNK], F32, name=f"v_raw{c}", tag=f"v_raw{c}")
+            nc.sync.dma_start(out=raw[:], in_=v_rows[:, :, c * CHUNK : (c + 1) * CHUNK])
+            v_raw.append(raw)
+        list2 = sb.tile([P, SLOTS // 16], U16)
+        nc.sync.dma_start(list2[:], offs2)
+        old_sb = sb.tile([P, T], F32)
+        nc.sync.dma_start(out=old_sb[:], in_=old)
+
+        ident = sb.tile([P, P], F32)
+        make_identity(nc, ident[:])
+        warm = sb.tile([P, 2], F32)
+        nc.vector.memset(warm[:, 0:1], 0.0)
+        nc.scalar.activation(out=warm[:, 1:2], in_=warm[:, 0:1], func=ACT.Exp)
+        minus_one = sb.tile([P, SLOTS], F32)
+        nc.vector.memset(minus_one[:], -1.0)
+        minus_rf = sb.tile([P, T], F32)
+        rg = sb.tile([P, T], F32)
+        s1 = sb.tile([P, T], F32)
+        for window in (minus_rf, rg, s1):
+            nc.vector.memset(window[:], 0.0)
+
+        q_grouped = sb.tile([P, P, PACK], BF16, align_bytes=64)
+        interleave(nc.vector.tensor_copy, q_grouped, q_raw)
+        q_codes, q_scales = quantize("q", q_grouped, P)
+        a = sb.tile([P, T], F32)
+        half_max = sb.tile([P, T // BANK], F32)
+        a_banks = [bank(f"a{h}") for h in range(T // BANK)]
+        for h, cols in enumerate(halves):
+            acc = a_banks[h]
+            nc.tensor.matmul_mx(out=acc[:], lhsT=q_codes[:].bitcast(FP8X4), lhsT_scale=q_scales[:],
+                                rhs=k_codes[h][:].bitcast(FP8X4), rhs_scale=k_scales[:, cols], start=True, stop=True)
+            nc.vector.tensor_reduce(out=half_max[:, h : h + 1], in_=acc[:], axis=AX.X, op=ALU.max)
+        minus_max = sb.tile([P, 1], F32)
+        nc.vector.tensor_reduce(out=minus_max[:], in_=half_max[:], axis=AX.X, op=ALU.max, negate=True)
+        nc.scalar.activation(out=a[:, halves[0]], in_=a_banks[0][:], func=ACT.Identity, bias=minus_max[:])
+        nc.vector.tensor_scalar(out=a[:, halves[1]], in0=a_banks[1][:], scalar1=minus_max[:], scalar2=None, op0=ALU.add)
+
+        def spread(tag, columns):
+            acc = bank(tag)
+            for j in range(PACK):
+                nc.tensor.transpose(acc[:, j * P : (j + 1) * P], columns[:, j : j + 1].to_broadcast([P, P]), ident[:])
+            return acc[:].rearrange("p (j n) -> p n j", j=PACK)
+
+        def by_word(ap):
+            return ap.rearrange("p (n j) -> p n j", j=PACK)
+
+        share_bank = spread("back0", share_cols)
+        share_lo = sb.tile([P, SLOTS // 2], F32)
+        nc.scalar.copy(out=by_word(share_lo[:]), in_=share_bank[:, 0 : P // 2, :])
+        fac_sb = sb.tile([P, T], F32)
+        for h, cols in enumerate(halves):
+            nc.scalar.activation(out=by_word(fac_sb[:, cols]), in_=spread(f"turned{h}", fac_cols[:, h, :]), func=ACT.Copy, scale=GAIN)
+
+        g_grouped = sb.tile([P, P, PACK], BF16, align_bytes=64)
+        interleave(nc.scalar.copy, g_grouped, g_raw)
+        g_codes, g_scales = quantize("g", g_grouped, P)
+
+        r = sb.tile([P, SLOTS], F32)
+        pieces = [(slice(i * 256, (i + 1) * 256), slice(i * 16, (i + 1) * 16)) for i in range(2)]
+        for slots, entries in pieces:
+            nc.scalar.activation(out=r[:, slots], in_=a[:].indirect(list1[:, entries]), func=ACT.Exp)
+        p = sb.tile([P, T], F32, name="p", tag="p")
+        z = sb.tile([P, 1], F32)
+        nc.scalar.activation(out=p[:], in_=a[:], func=ACT.Exp, accum_out=z[:])
+
+        v_grouped = []
+        for c in range(T // CHUNK):
+            grouped = sb.tile([P, CHUNK, PACK], BF16, name=f"v_grouped{c}", align_bytes=64)
+            interleave(nc.vector.tensor_copy if c == 0 else nc.scalar.copy, grouped, v_raw[c])
+            v_grouped.append(grouped)
+        share_hi = sb.tile([P, SLOTS // 2], F32, name="share_hi", tag=f"v_raw{T // CHUNK - 1}")
+        nc.scalar.copy(out=by_word(share_hi[:]), in_=share_bank[:, P // 2 : P, :])
+        share_pieces = [share_lo, share_hi]
+
+        for slots, entries in pieces:
+            nc.vector.tensor_tensor(minus_rf[:].indirect(list1[:, entries]), r[:, slots], minus_one[:, slots], ALU.mult)
+        rz = sb.tile([P, 1], F32)
+        nc.vector.reciprocal(out=rz[:], in_=z[:])
+        nc.vector.tensor_tensor(rg[:].indirect(list2[:, pieces[0][1]]), r[:, pieces[0][0]], share_lo[:], ALU.mult)
+
+        c_banks = [bank(f"c{h}") for h in range(T // BANK)]
+        for c in range(T // CHUNK):
+            v_codes, v_scales = quantize(f"v{c}", v_grouped[c], CHUNK)
+            h, part = divmod(c, BANK // CHUNK)
+            nc.tensor.matmul_mx(out=c_banks[h][:, part * CHUNK : (part + 1) * CHUNK], lhsT=g_codes[:].bitcast(FP8X4),
+                                lhsT_scale=g_scales[:], rhs=v_codes[:].bitcast(FP8X4), rhs_scale=v_scales[:],
+                                start=True, stop=True)
+        nc.vector.tensor_tensor(rg[:].indirect(list2[:, pieces[1][1]]), r[:, pieces[1][0]], share_hi[:], ALU.mult)
+        drg = sb.tile([P, T], F32)
+        for h, cols in enumerate(halves):
+            nc.vector.scalar_tensor_tensor(out=drg[:, cols], in0=c_banks[h][:], scalar=rz[:], in1=fac_sb[:, cols],
+                                           op0=ALU.mult, op1=ALU.mult)
+
+        w_turned = [bank(f"turned{h}") for h in range(T // BANK)]
+        for i, term in enumerate((p, minus_rf, rg)):
+            for h, cols in enumerate(halves):
+                turn(w_turned[h], term[:, cols], i == 0, i == 2)
+        w_turned_sb = sb.tile([P, T], F32, name="w_turned_sb", tag="w_turned_sb")
+        w = [bank(f"back{h}") for h in range(T // BANK)]
+        for h, cols in enumerate(halves):
+            nc.scalar.copy(out=w_turned_sb[:, cols], in_=w_turned[h][:])
+            turn(w[h], w_turned_sb[:, cols], True, True)
+
+        dra_share = sb.tile([P, SLOTS], F32)
+        for (slots, entries), share_piece in zip(pieces, share_pieces):
+            nc.vector.tensor_tensor(dra_share[:, slots], drg[:].indirect(list2[:, entries]), share_piece[:], ALU.mult)
+        drf = sb.tile([P, T], F32, name="drf", tag="w_turned_sb")
+        nc.scalar.activation(out=drf[:], in_=drg[:], func=ACT.Copy, scale=-1.0)
+
+        terms = sb.tile([P, T], F32)
+        half_sum = sb.tile([P, T // BANK], F32)
+        for h, cols in enumerate(halves):
+            nc.vector.scalar_tensor_tensor(out=terms[:, cols], in0=w[h][:], scalar=rz[:], in1=drg[:, cols],
+                                           op0=ALU.mult, op1=ALU.mult, accum_out=half_sum[:, h : h + 1])
+        dz = sb.tile([P, 1], F32)
+        nc.vector.tensor_reduce(out=dz[:], in_=half_sum[:], axis=AX.X, op=ALU.add, negate=True)
+        dpp = sb.tile([P, T], F32)
+        for cols in halves:
+            nc.vector.scalar_tensor_tensor(out=dpp[:, cols], in0=drg[:, cols], scalar=dz[:], in1=p[:, cols],
+                                           op0=ALU.add, op1=ALU.mult)
+        dr = sb.tile([P, SLOTS], F32, name="dr", tag="p")
+        nc.vector.tensor_tensor(dr[:], drf[:].indirect(list1[:]), dra_share[:], ALU.add)
+        nc.vector.tensor_tensor(s1[:].indirect(list1[:]), dr[:], r[:], ALU.mult)
+
+        b_turned = [bank(f"a{h}") for h in range(T // BANK)]
+        for i, term in enumerate((old_sb, dpp)):
+            for h, cols in enumerate(halves):
+                turn(b_turned[h], term[:, cols], i == 0, i == 1)
+        b_turned_sb = sb.tile([P, T], F32)
+        b = [bank(f"c{h}") for h in range(T // BANK)]
+        for h, cols in enumerate(halves):
+            nc.scalar.copy(out=b_turned_sb[:, cols], in_=b_turned[h][:])
+            turn(b[h], b_turned_sb[:, cols], True, True)
+
+        result = sb.tile([P, T], F32)
+        for c in range(T // CHUNK):
+            h, part = divmod(c, BANK // CHUNK)
+            cols = slice(c * CHUNK, (c + 1) * CHUNK)
+            nc.vector.tensor_tensor(result[:, cols], b[h][:, part * CHUNK : (part + 1) * CHUNK], s1[:, cols], ALU.add)
+            nc.sync.dma_start(out=out[:, cols], in_=result[:, cols])

@@ -56,30 +56,29 @@ def tile_attend_bpassedon_heads_kernel(tc, query, keys_words, keys_scales, gout,
         q_raw = sb.tile([P, PACK, P], F32)
         nc.sync.dma_start(out=q_raw[:], in_=query.rearrange("(p j) w -> p j w", j=PACK))
         for quad in range(4):
-            nc.scalar.dma_start(out=k_scales[32 * quad : 32 * quad + 4, :].bitcast(I32),
-                                in_=keys_scales[0, 4 * quad : 4 * quad + 4, :].bitcast(I32))
-        k_words = keys_words[0].rearrange("p n t -> p (n t)").bitcast(I32)
-        k_codes = []
-        for h, cols in enumerate(halves):
-            codes = sb.tile([P, BANK], U32, name=f"k_codes{h}", align_bytes=64)
-            nc.sync.dma_start(out=codes[:].bitcast(I32), in_=k_words[:, cols])
-            k_codes.append(codes)
-        fac_cols = sb.tile([P, T // BANK, PACK], F32)
-        nc.sync.dma_start(out=fac_cols[:], in_=fac[0].rearrange("(h p j) -> p h j", p=P, j=PACK))
-        share_cols = sb.tile([P, PACK], F32)
-        nc.sync.dma_start(out=share_cols[:], in_=share[0].rearrange("(p j) -> p j", j=PACK))
-        list1 = sb.tile([P, SLOTS // 16], U16)
-        nc.sync.dma_start(list1[:], offs)
+            nc.sync.dma_start(out=k_scales[32 * quad : 32 * quad + 4, :].bitcast(I32),
+                              in_=keys_scales[0, 4 * quad : 4 * quad + 4, :].bitcast(I32))
+        k_codes = sb.tile([P, T], U32, align_bytes=64)
+        nc.sync.dma_start(out=k_codes[:].bitcast(I32), in_=keys_words[0].rearrange("p n t -> p (n t)").bitcast(I32))
         g_raw = sb.tile([P, PACK, P], F32)
         nc.sync.dma_start(out=g_raw[:], in_=gout.rearrange("(p j) w -> p j w", j=PACK))
         v_rows = vals.rearrange("(p j) w -> p j w", j=PACK)
-        v_raw = []
-        for c in range(T // CHUNK):
-            raw = sb.tile([P, PACK, CHUNK], F32, name=f"v_raw{c}", tag=f"v_raw{c}")
-            nc.sync.dma_start(out=raw[:], in_=v_rows[:, :, c * CHUNK : (c + 1) * CHUNK])
-            v_raw.append(raw)
+        v_raw = [sb.tile([P, PACK, CHUNK], F32, name=f"v_raw{c}", tag=f"v_raw{c}") for c in range(T // CHUNK)]
+
+        def load_vals(c):
+            nc.sync.dma_start(out=v_raw[c][:], in_=v_rows[:, :, c * CHUNK : (c + 1) * CHUNK])
+
+        load_vals(0)
+        list1 = sb.tile([P, SLOTS // 16], U16)
+        nc.sync.dma_start(list1[:], offs)
+        share_cols = sb.tile([P, PACK], F32)
+        nc.sync.dma_start(out=share_cols[:], in_=share[0].rearrange("(p j) -> p j", j=PACK))
+        for c in range(1, T // CHUNK):
+            load_vals(c)
         list2 = sb.tile([P, SLOTS // 16], U16)
         nc.sync.dma_start(list2[:], offs2)
+        fac_sb = sb.tile([P, T], F32)
+        nc.sync.dma_start(out=fac_sb[:], in_=fac[0].partition_broadcast(P))
         old_sb = sb.tile([P, T], F32)
         nc.sync.dma_start(out=old_sb[:], in_=old)
 
@@ -105,12 +104,11 @@ def tile_attend_bpassedon_heads_kernel(tc, query, keys_words, keys_scales, gout,
         for h, cols in enumerate(halves):
             acc = a_banks[h]
             nc.tensor.matmul_mx(out=acc[:], lhsT=q_codes[:].bitcast(FP8X4), lhsT_scale=q_scales[:],
-                                rhs=k_codes[h][:].bitcast(FP8X4), rhs_scale=k_scales[:, cols], start=True, stop=True)
-            nc.vector.tensor_reduce(out=half_max[:, h : h + 1], in_=acc[:], axis=AX.X, op=ALU.max)
+                                rhs=k_codes[:, cols].bitcast(FP8X4), rhs_scale=k_scales[:, cols], start=True, stop=True)
+            nc.vector.tensor_scalar(out=a[:, cols], in0=acc[:], scalar1=1.0, scalar2=None, op0=ALU.mult, op1=ALU.max,
+                                    accum_out=half_max[:, h : h + 1])
         minus_max = sb.tile([P, 1], F32)
         nc.vector.tensor_reduce(out=minus_max[:], in_=half_max[:], axis=AX.X, op=ALU.max, negate=True)
-        nc.scalar.activation(out=a[:, halves[0]], in_=a_banks[0][:], func=ACT.Identity, bias=minus_max[:])
-        nc.vector.tensor_scalar(out=a[:, halves[1]], in0=a_banks[1][:], scalar1=minus_max[:], scalar2=None, op0=ALU.add)
 
         def spread(tag, columns):
             acc = bank(tag)
@@ -122,37 +120,38 @@ def tile_attend_bpassedon_heads_kernel(tc, query, keys_words, keys_scales, gout,
             return ap.rearrange("p (n j) -> p n j", j=PACK)
 
         share_bank = spread("back0", share_cols)
-        share_lo = sb.tile([P, SLOTS // 2], F32)
-        nc.scalar.copy(out=by_word(share_lo[:]), in_=share_bank[:, 0 : P // 2, :])
-        fac_sb = sb.tile([P, T], F32)
-        for h, cols in enumerate(halves):
-            nc.scalar.activation(out=by_word(fac_sb[:, cols]), in_=spread(f"turned{h}", fac_cols[:, h, :]), func=ACT.Copy, scale=GAIN)
 
         g_grouped = sb.tile([P, P, PACK], BF16, align_bytes=64)
         interleave(nc.scalar.copy, g_grouped, g_raw)
         g_codes, g_scales = quantize("g", g_grouped, P)
 
+        v_grouped = [sb.tile([P, CHUNK, PACK], BF16, name="v_grouped0", align_bytes=64)]
+        interleave(nc.scalar.copy, v_grouped[0], v_raw[0])
+
         r = sb.tile([P, SLOTS], F32)
         pieces = [(slice(i * 256, (i + 1) * 256), slice(i * 16, (i + 1) * 16)) for i in range(2)]
+        a_listed = sb.tile([P, SLOTS], F32, name="a_listed", tag="v_grouped1", align_bytes=64)
         for slots, entries in pieces:
-            nc.scalar.activation(out=r[:, slots], in_=a[:].indirect(list1[:, entries]), func=ACT.Exp)
-        p = sb.tile([P, T], F32, name="p", tag="p")
-        z = sb.tile([P, 1], F32)
-        nc.scalar.activation(out=p[:], in_=a[:], func=ACT.Exp, accum_out=z[:])
+            nc.vector.tensor_copy(a_listed[:, slots], a[:].indirect(list1[:, entries]))
+            nc.scalar.activation(out=r[:, slots], in_=a_listed[:, slots], func=ACT.Exp, bias=minus_max[:])
 
-        v_grouped = []
-        for c in range(T // CHUNK):
-            grouped = sb.tile([P, CHUNK, PACK], BF16, name=f"v_grouped{c}", align_bytes=64)
-            interleave(nc.vector.tensor_copy if c == 0 else nc.scalar.copy, grouped, v_raw[c])
+        share_lo = sb.tile([P, SLOTS // 2], F32, name="share_lo", tag="share_lo")
+        nc.scalar.copy(out=by_word(share_lo[:]), in_=share_bank[:, 0 : P // 2, :])
+        for c in range(1, T // CHUNK):
+            grouped = sb.tile([P, CHUNK, PACK], BF16, name=f"v_grouped{c}", tag=f"v_grouped{c}", align_bytes=64)
+            interleave(nc.scalar.copy, grouped, v_raw[c])
             v_grouped.append(grouped)
         share_hi = sb.tile([P, SLOTS // 2], F32, name="share_hi", tag=f"v_raw{T // CHUNK - 1}")
         nc.scalar.copy(out=by_word(share_hi[:]), in_=share_bank[:, P // 2 : P, :])
         share_pieces = [share_lo, share_hi]
+        p = sb.tile([P, T], F32, name="p", tag="v_raw2")
+        z = sb.tile([P, 1], F32)
+        nc.scalar.activation(out=p[:], in_=a[:], func=ACT.Exp, bias=minus_max[:], accum_out=z[:])
+        z_gain = sb.tile([P, 1], F32)
+        nc.scalar.mul(out=z_gain[:], in_=z[:], mul=1.0 / GAIN)
 
         for slots, entries in pieces:
             nc.vector.tensor_tensor(minus_rf[:].indirect(list1[:, entries]), r[:, slots], minus_one[:, slots], ALU.mult)
-        rz = sb.tile([P, 1], F32)
-        nc.vector.reciprocal(out=rz[:], in_=z[:])
         nc.vector.tensor_tensor(rg[:].indirect(list2[:, pieces[0][1]]), r[:, pieces[0][0]], share_lo[:], ALU.mult)
 
         c_banks = [bank(f"c{h}") for h in range(T // BANK)]
@@ -163,13 +162,15 @@ def tile_attend_bpassedon_heads_kernel(tc, query, keys_words, keys_scales, gout,
                                 lhsT_scale=g_scales[:], rhs=v_codes[:].bitcast(FP8X4), rhs_scale=v_scales[:],
                                 start=True, stop=True)
         nc.vector.tensor_tensor(rg[:].indirect(list2[:, pieces[1][1]]), r[:, pieces[1][0]], share_hi[:], ALU.mult)
+        rz = sb.tile([P, 1], F32)
+        nc.vector.reciprocal(out=rz[:], in_=z_gain[:])
         drg = sb.tile([P, T], F32)
         for h, cols in enumerate(halves):
             nc.vector.scalar_tensor_tensor(out=drg[:, cols], in0=c_banks[h][:], scalar=rz[:], in1=fac_sb[:, cols],
                                            op0=ALU.mult, op1=ALU.mult)
 
         w_turned = [bank(f"turned{h}") for h in range(T // BANK)]
-        for i, term in enumerate((p, minus_rf, rg)):
+        for i, term in enumerate((minus_rf, p, rg)):
             for h, cols in enumerate(halves):
                 turn(w_turned[h], term[:, cols], i == 0, i == 2)
         w_turned_sb = sb.tile([P, T], F32, name="w_turned_sb", tag="w_turned_sb")
@@ -190,12 +191,13 @@ def tile_attend_bpassedon_heads_kernel(tc, query, keys_words, keys_scales, gout,
             nc.vector.scalar_tensor_tensor(out=terms[:, cols], in0=w[h][:], scalar=rz[:], in1=drg[:, cols],
                                            op0=ALU.mult, op1=ALU.mult, accum_out=half_sum[:, h : h + 1])
         dz = sb.tile([P, 1], F32)
-        nc.vector.tensor_reduce(out=dz[:], in_=half_sum[:], axis=AX.X, op=ALU.add, negate=True)
+        nc.vector.tensor_scalar(out=dz[:], in0=half_sum[:, 0:1], scalar1=half_sum[:, 1:2], scalar2=-1.0 / GAIN,
+                                op0=ALU.add, op1=ALU.mult)
         dpp = sb.tile([P, T], F32)
         for cols in halves:
             nc.vector.scalar_tensor_tensor(out=dpp[:, cols], in0=drg[:, cols], scalar=dz[:], in1=p[:, cols],
                                            op0=ALU.add, op1=ALU.mult)
-        dr = sb.tile([P, SLOTS], F32, name="dr", tag="p")
+        dr = sb.tile([P, SLOTS], F32, name="dr", tag="v_raw2")
         nc.vector.tensor_tensor(dr[:], drf[:].indirect(list1[:]), dra_share[:], ALU.add)
         nc.vector.tensor_tensor(s1[:].indirect(list1[:]), dr[:], r[:], ALU.mult)
 

@@ -169,6 +169,9 @@ def tile_attend_bpassedon_heads_kernel(tc, query, keys_words, keys_scales, gout,
             nc.vector.scalar_tensor_tensor(out=drg[:, cols], in0=c_banks[h][:], scalar=rz[:], in1=fac_sb[:, cols],
                                            op0=ALU.mult, op1=ALU.mult)
 
+        u_first = sb.tile([P, CHUNK], F32)
+        nc.gpsimd.tensor_tensor(u_first[:], drg[:, 0:CHUNK], p[:, 0:CHUNK], ALU.mult)
+
         w_turned = [bank(f"turned{h}") for h in range(T // BANK)]
         for i, term in enumerate((minus_rf, p, rg)):
             for h, cols in enumerate(halves):
@@ -182,6 +185,8 @@ def tile_attend_bpassedon_heads_kernel(tc, query, keys_words, keys_scales, gout,
         dra_share = sb.tile([P, SLOTS], F32)
         for (slots, entries), share_piece in zip(pieces, share_pieces):
             nc.vector.tensor_tensor(dra_share[:, slots], drg[:].indirect(list2[:, entries]), share_piece[:], ALU.mult)
+        u_mid = sb.tile([P, 2 * CHUNK], F32, name="u_mid", tag=f"v_raw{T // CHUNK - 1}")
+        nc.gpsimd.tensor_tensor(u_mid[:], drg[:, CHUNK : 3 * CHUNK], p[:, CHUNK : 3 * CHUNK], ALU.mult)
         drf = sb.tile([P, T], F32, name="drf", tag="w_turned_sb")
         nc.scalar.activation(out=drf[:], in_=drg[:], func=ACT.Copy, scale=-1.0)
 
@@ -190,21 +195,28 @@ def tile_attend_bpassedon_heads_kernel(tc, query, keys_words, keys_scales, gout,
         for h, cols in enumerate(halves):
             nc.vector.scalar_tensor_tensor(out=terms[:, cols], in0=w[h][:], scalar=rz[:], in1=drg[:, cols],
                                            op0=ALU.mult, op1=ALU.mult, accum_out=half_sum[:, h : h + 1])
+        u_last = sb.tile([P, CHUNK], F32)
+        nc.vector.tensor_tensor(u_last[:], drg[:, 3 * CHUNK : T], p[:, 3 * CHUNK : T], ALU.mult)
         dz = sb.tile([P, 1], F32)
         nc.vector.tensor_scalar(out=dz[:], in0=half_sum[:, 0:1], scalar1=half_sum[:, 1:2], scalar2=-1.0 / GAIN,
                                 op0=ALU.add, op1=ALU.mult)
-        dpp = sb.tile([P, T], F32)
+        dzp = sb.tile([P, T], F32)
         for cols in halves:
-            nc.vector.scalar_tensor_tensor(out=dpp[:, cols], in0=drg[:, cols], scalar=dz[:], in1=p[:, cols],
-                                           op0=ALU.add, op1=ALU.mult)
-        dr = sb.tile([P, SLOTS], F32, name="dr", tag="v_raw2")
+            nc.scalar.activation(out=dzp[:, cols], in_=p[:, cols], func=ACT.Copy, scale=dz[:])
+        dr = sb.tile([P, SLOTS], F32)
         nc.vector.tensor_tensor(dr[:], drf[:].indirect(list1[:]), dra_share[:], ALU.add)
         nc.vector.tensor_tensor(s1[:].indirect(list1[:]), dr[:], r[:], ALU.mult)
 
         b_turned = [bank(f"a{h}") for h in range(T // BANK)]
-        for i, term in enumerate((old_sb, dpp)):
-            for h, cols in enumerate(halves):
-                turn(b_turned[h], term[:, cols], i == 0, i == 1)
+        for h, cols in enumerate(halves):
+            turn(b_turned[h], old_sb[:, cols], True, False)
+        for tile_, first in ((u_first, 0), (u_mid, CHUNK), (u_last, 3 * CHUNK)):
+            for j in range(tile_.shape[1] // P):
+                h, at = divmod(first + j * P, BANK)
+                nc.tensor.matmul(b_turned[h][:, at : at + P], lhsT=tile_[:, j * P : (j + 1) * P], rhs=ident[:],
+                                 is_transpose=True, start=False, stop=False)
+        for h, cols in enumerate(halves):
+            turn(b_turned[h], dzp[:, cols], False, True)
         b_turned_sb = sb.tile([P, T], F32)
         b = [bank(f"c{h}") for h in range(T // BANK)]
         for h, cols in enumerate(halves):
@@ -212,7 +224,12 @@ def tile_attend_bpassedon_heads_kernel(tc, query, keys_words, keys_scales, gout,
             turn(b[h], b_turned_sb[:, cols], True, True)
 
         result = sb.tile([P, T], F32)
-        for c in range(T // CHUNK):
+        last = slice(T - CHUNK, T)
+        b_last = sb.tile([P, CHUNK], F32)
+        nc.scalar.copy(out=b_last[:], in_=b[1][:, BANK - CHUNK : BANK])
+        nc.gpsimd.tensor_tensor(result[:, last], b_last[:], s1[:, last], ALU.add)
+        nc.scalar.dma_start(out=out[:, last], in_=result[:, last])
+        for c in range(T // CHUNK - 1):
             h, part = divmod(c, BANK // CHUNK)
             cols = slice(c * CHUNK, (c + 1) * CHUNK)
             nc.vector.tensor_tensor(result[:, cols], b[h][:, part * CHUNK : (part + 1) * CHUNK], s1[:, cols], ALU.add)

@@ -37,7 +37,7 @@ def tile_attend_bpassedon_heads_kernel(tc, query, keys_words, keys_scales, gout,
             return ps.tile([P, BANK], F32, name=tag, tag=tag)
 
         def interleave(copy, grouped, raw):
-            copy(out=grouped[:].rearrange("p (c i) t -> p c t i", i=4), in_=raw[:].rearrange("p t (c i) -> p c t i", i=4))
+            copy(out=grouped[:].rearrange("p (c i) t -> p c t i", i=4), in_=raw.rearrange("p t (c i) -> p c t i", i=4))
 
         def quantize(name, grouped, width):
             codes = sb.tile([P, width], U32, name=name + "_codes", align_bytes=64)
@@ -52,16 +52,16 @@ def tile_attend_bpassedon_heads_kernel(tc, query, keys_words, keys_scales, gout,
                                  start=(first and j == 0), stop=(last and j == BANK // P - 1))
 
         k_scales = sb.tile([P, T], U8, align_bytes=64)
-        nc.vector.memset(k_scales[:].bitcast(I32), 0)
+        nc.gpsimd.memset(k_scales[:].bitcast(I32), 0)
         q_raw = sb.tile([P, PACK, P], F32)
         nc.sync.dma_start(out=q_raw[:], in_=query.rearrange("(p j) w -> p j w", j=PACK))
+        k_codes = sb.tile([P, T], U32, align_bytes=64)
+        nc.sync.dma_start(out=k_codes[:].bitcast(I32), in_=keys_words[0].rearrange("p n t -> p (n t)").bitcast(I32))
         for quad in range(4):
             nc.sync.dma_start(out=k_scales[32 * quad : 32 * quad + 4, :].bitcast(I32),
                               in_=keys_scales[0, 4 * quad : 4 * quad + 4, :].bitcast(I32))
-        k_codes = sb.tile([P, T], U32, align_bytes=64)
-        nc.sync.dma_start(out=k_codes[:].bitcast(I32), in_=keys_words[0].rearrange("p n t -> p (n t)").bitcast(I32))
-        g_raw = sb.tile([P, PACK, P], F32)
-        nc.sync.dma_start(out=g_raw[:], in_=gout.rearrange("(p j) w -> p j w", j=PACK))
+        list1 = sb.tile([P, SLOTS // 16], U16)
+        nc.sync.dma_start(list1[:], offs)
         v_rows = vals.rearrange("(p j) w -> p j w", j=PACK)
         v_raw = [sb.tile([P, PACK, CHUNK], F32, name=f"v_raw{c}", tag=f"v_raw{c}") for c in range(T // CHUNK)]
 
@@ -69,8 +69,8 @@ def tile_attend_bpassedon_heads_kernel(tc, query, keys_words, keys_scales, gout,
             nc.sync.dma_start(out=v_raw[c][:], in_=v_rows[:, :, c * CHUNK : (c + 1) * CHUNK])
 
         load_vals(0)
-        list1 = sb.tile([P, SLOTS // 16], U16)
-        nc.sync.dma_start(list1[:], offs)
+        g_raw = sb.tile([P, PACK, P], F32)
+        nc.sync.dma_start(out=g_raw[:], in_=gout.rearrange("(p j) w -> p j w", j=PACK))
         share_cols = sb.tile([P, PACK], F32)
         nc.sync.dma_start(out=share_cols[:], in_=share[0].rearrange("(p j) -> p j", j=PACK))
         for c in range(1, T // CHUNK):
@@ -84,10 +84,7 @@ def tile_attend_bpassedon_heads_kernel(tc, query, keys_words, keys_scales, gout,
 
         ident = sb.tile([P, P], F32)
         make_identity(nc, ident[:])
-        warm = sb.tile([P, 2], F32)
-        nc.vector.memset(warm[:, 0:1], 0.0)
-        nc.scalar.activation(out=warm[:, 1:2], in_=warm[:, 0:1], func=ACT.Exp)
-        minus_one = sb.tile([P, SLOTS], F32)
+        minus_one = sb.tile([P, SLOTS // 2], F32)
         nc.vector.memset(minus_one[:], -1.0)
         minus_rf = sb.tile([P, T], F32)
         rg = sb.tile([P, T], F32)
@@ -96,7 +93,7 @@ def tile_attend_bpassedon_heads_kernel(tc, query, keys_words, keys_scales, gout,
             nc.vector.memset(window[:], 0.0)
 
         q_grouped = sb.tile([P, P, PACK], BF16, align_bytes=64)
-        interleave(nc.vector.tensor_copy, q_grouped, q_raw)
+        interleave(nc.vector.tensor_copy, q_grouped, q_raw[:])
         q_codes, q_scales = quantize("q", q_grouped, P)
         a = sb.tile([P, T], F32)
         half_max = sb.tile([P, T // BANK], F32)
@@ -121,26 +118,32 @@ def tile_attend_bpassedon_heads_kernel(tc, query, keys_words, keys_scales, gout,
 
         share_bank = spread("back0", share_cols)
 
-        g_grouped = sb.tile([P, P, PACK], BF16, align_bytes=64)
-        interleave(nc.scalar.copy, g_grouped, g_raw)
-        g_codes, g_scales = quantize("g", g_grouped, P)
+        v_grouped = []
 
-        v_grouped = [sb.tile([P, CHUNK, PACK], BF16, name="v_grouped0", align_bytes=64)]
-        interleave(nc.scalar.copy, v_grouped[0], v_raw[0])
+        def group_vals(first, width, tag):
+            grouped = sb.tile([P, width, PACK], BF16, name=f"v_grouped{first}", tag=tag, align_bytes=64)
+            c, at = divmod(first, CHUNK)
+            interleave(nc.scalar.copy, grouped, v_raw[c][:, :, at : at + width])
+            v_grouped.append((first, width, grouped))
+
+        group_vals(0, P, "v_grouped_first")
+        g_grouped = sb.tile([P, P, PACK], BF16, align_bytes=64)
+        interleave(lambda out, in_: nc.scalar.activation(out=out, in_=in_, func=ACT.Copy), g_grouped, g_raw[:])
+        g_codes, g_scales = quantize("g", g_grouped, P)
 
         r = sb.tile([P, SLOTS], F32)
         pieces = [(slice(i * 256, (i + 1) * 256), slice(i * 16, (i + 1) * 16)) for i in range(2)]
-        a_listed = sb.tile([P, SLOTS], F32, name="a_listed", tag="v_grouped1", align_bytes=64)
-        for slots, entries in pieces:
-            nc.vector.tensor_copy(a_listed[:, slots], a[:].indirect(list1[:, entries]))
-            nc.scalar.activation(out=r[:, slots], in_=a_listed[:, slots], func=ACT.Exp, bias=minus_max[:])
+        for i, (slots, entries) in enumerate(pieces):
+            a_listed = sb.tile([P, SLOTS // 2], F32, name=f"a_listed{i}", tag=f"a_listed{i}", align_bytes=64)
+            nc.vector.tensor_copy(a_listed[:], a[:].indirect(list1[:, entries]))
+            nc.scalar.activation(out=r[:, slots], in_=a_listed[:], func=ACT.Exp, bias=minus_max[:])
 
         share_lo = sb.tile([P, SLOTS // 2], F32, name="share_lo", tag="share_lo")
         nc.scalar.copy(out=by_word(share_lo[:]), in_=share_bank[:, 0 : P // 2, :])
-        for c in range(1, T // CHUNK):
-            grouped = sb.tile([P, CHUNK, PACK], BF16, name=f"v_grouped{c}", tag=f"v_grouped{c}", align_bytes=64)
-            interleave(nc.scalar.copy, grouped, v_raw[c])
-            v_grouped.append(grouped)
+        group_vals(P, P, "a_listed0")
+        group_vals(CHUNK, CHUNK, "a_listed1")
+        for c in range(2, T // CHUNK):
+            group_vals(c * CHUNK, CHUNK, f"v_grouped{c}")
         share_hi = sb.tile([P, SLOTS // 2], F32, name="share_hi", tag=f"v_raw{T // CHUNK - 1}")
         nc.scalar.copy(out=by_word(share_hi[:]), in_=share_bank[:, P // 2 : P, :])
         share_pieces = [share_lo, share_hi]
@@ -151,14 +154,14 @@ def tile_attend_bpassedon_heads_kernel(tc, query, keys_words, keys_scales, gout,
         nc.scalar.mul(out=z_gain[:], in_=z[:], mul=1.0 / GAIN)
 
         for slots, entries in pieces:
-            nc.vector.tensor_tensor(minus_rf[:].indirect(list1[:, entries]), r[:, slots], minus_one[:, slots], ALU.mult)
+            nc.vector.tensor_tensor(minus_rf[:].indirect(list1[:, entries]), r[:, slots], minus_one[:], ALU.mult)
         nc.vector.tensor_tensor(rg[:].indirect(list2[:, pieces[0][1]]), r[:, pieces[0][0]], share_lo[:], ALU.mult)
 
         c_banks = [bank(f"c{h}") for h in range(T // BANK)]
-        for c in range(T // CHUNK):
-            v_codes, v_scales = quantize(f"v{c}", v_grouped[c], CHUNK)
-            h, part = divmod(c, BANK // CHUNK)
-            nc.tensor.matmul_mx(out=c_banks[h][:, part * CHUNK : (part + 1) * CHUNK], lhsT=g_codes[:].bitcast(FP8X4),
+        for first, width, grouped in v_grouped:
+            v_codes, v_scales = quantize(f"v{first}", grouped, width)
+            h, at = divmod(first, BANK)
+            nc.tensor.matmul_mx(out=c_banks[h][:, at : at + width], lhsT=g_codes[:].bitcast(FP8X4),
                                 lhsT_scale=g_scales[:], rhs=v_codes[:].bitcast(FP8X4), rhs_scale=v_scales[:],
                                 start=True, stop=True)
         nc.vector.tensor_tensor(rg[:].indirect(list2[:, pieces[1][1]]), r[:, pieces[1][0]], share_hi[:], ALU.mult)
@@ -176,18 +179,18 @@ def tile_attend_bpassedon_heads_kernel(tc, query, keys_words, keys_scales, gout,
         for i, term in enumerate((minus_rf, p, rg)):
             for h, cols in enumerate(halves):
                 turn(w_turned[h], term[:, cols], i == 0, i == 2)
-        w_turned_sb = sb.tile([P, T], F32, name="w_turned_sb", tag="w_turned_sb")
         w = [bank(f"back{h}") for h in range(T // BANK)]
         for h, cols in enumerate(halves):
-            nc.scalar.copy(out=w_turned_sb[:, cols], in_=w_turned[h][:])
-            turn(w[h], w_turned_sb[:, cols], True, True)
+            w_turned_sb = sb.tile([P, BANK], F32, name=f"w_turned_sb{h}", tag=f"w_turned_sb{h}")
+            nc.scalar.copy(out=w_turned_sb[:], in_=w_turned[h][:])
+            turn(w[h], w_turned_sb[:], True, True)
 
         dra_share = sb.tile([P, SLOTS], F32)
         for (slots, entries), share_piece in zip(pieces, share_pieces):
             nc.vector.tensor_tensor(dra_share[:, slots], drg[:].indirect(list2[:, entries]), share_piece[:], ALU.mult)
         u_mid = sb.tile([P, 2 * CHUNK], F32, name="u_mid", tag=f"v_raw{T // CHUNK - 1}")
         nc.gpsimd.tensor_tensor(u_mid[:], drg[:, CHUNK : 3 * CHUNK], p[:, CHUNK : 3 * CHUNK], ALU.mult)
-        drf = sb.tile([P, T], F32, name="drf", tag="w_turned_sb")
+        drf = sb.tile([P, T], F32, name="drf", tag="w_turned_sb0")
         nc.scalar.activation(out=drf[:], in_=drg[:], func=ACT.Copy, scale=-1.0)
 
         terms = sb.tile([P, T], F32)
@@ -198,8 +201,8 @@ def tile_attend_bpassedon_heads_kernel(tc, query, keys_words, keys_scales, gout,
         u_last = sb.tile([P, CHUNK], F32)
         nc.vector.tensor_tensor(u_last[:], drg[:, 3 * CHUNK : T], p[:, 3 * CHUNK : T], ALU.mult)
         dz = sb.tile([P, 1], F32)
-        nc.vector.tensor_scalar(out=dz[:], in0=half_sum[:, 0:1], scalar1=half_sum[:, 1:2], scalar2=-1.0 / GAIN,
-                                op0=ALU.add, op1=ALU.mult)
+        half_dz = sb.tile([P, T // BANK], F32)
+        nc.scalar.activation(out=half_dz[:], in_=half_sum[:], func=ACT.Copy, scale=-1.0 / GAIN, accum_out=dz[:])
         dzp = sb.tile([P, T], F32)
         for cols in halves:
             nc.scalar.activation(out=dzp[:, cols], in_=p[:, cols], func=ACT.Copy, scale=dz[:])

@@ -227,12 +227,11 @@ def tile_attend_bpassedon_heads_kernel(tc, query, keys_words, keys_scales, gout,
             turn(b[h], b_turned_sb[:, cols], True, True)
 
         result = sb.tile([P, T], F32)
-        last = slice(T - CHUNK, T)
-        b_last = sb.tile([P, CHUNK], F32)
-        nc.scalar.copy(out=b_last[:], in_=b[1][:, BANK - CHUNK : BANK])
-        nc.gpsimd.tensor_tensor(result[:, last], b_last[:], s1[:, last], ALU.add)
-        nc.scalar.dma_start(out=out[:, last], in_=result[:, last])
-        for c in range(T // CHUNK - 1):
+        b_first = sb.tile([P, CHUNK], F32)
+        nc.scalar.copy(out=b_first[:], in_=b[0][:, 0:CHUNK])
+        nc.gpsimd.tensor_tensor(result[:, 0:CHUNK], b_first[:], s1[:, 0:CHUNK], ALU.add)
+        nc.scalar.dma_start(out=out[:, 0:CHUNK], in_=result[:, 0:CHUNK])
+        for c in range(1, T // CHUNK):
             h, part = divmod(c, BANK // CHUNK)
             cols = slice(c * CHUNK, (c + 1) * CHUNK)
             nc.vector.tensor_tensor(result[:, cols], b[h][:, part * CHUNK : (part + 1) * CHUNK], s1[:, cols], ALU.add)

from contextlib import ExitStack

import concourse.mybir as mybir
from concourse.masks import make_identity

F32 = mybir.dt.float32
BF16 = mybir.dt.bfloat16
I32 = mybir.dt.int32
U32 = mybir.dt.uint32
U16 = mybir.dt.uint16
U8 = mybir.dt.uint8
FP8X4 = mybir.dt.float8_e4m3fn_x4
ALU = mybir.AluOpType
ACT = mybir.ActivationFunctionType
AX = mybir.AxisListType

P = 128
PACK = 4
T = 1024
SLOTS = 512
BANK = 512
CHUNK = 256
GAIN = 1024.0

FLOPS = 2 * 2 * 512 * 128 * 1024


def tile_attend_bpassedon_heads_kernel(tc, query, keys_words, keys_scales, gout, vals, share, fac, old, offs, offs2, out):
    nc = tc.nc
    halves = [slice(h * BANK, (h + 1) * BANK) for h in range(T // BANK)]

    with ExitStack() as ctx:
        sb = ctx.enter_context(tc.tile_pool(name="sb", bufs=1))
        ps = ctx.enter_context(tc.psum_pool(name="ps", bufs=1))

        def bank(tag):
            return ps.tile([P, BANK], F32, name=tag, tag=tag)

        def interleave(copy, grouped, raw):
            copy(out=grouped[:].rearrange("p (c i) t -> p c t i", i=4), in_=raw.rearrange("p t (c i) -> p c t i", i=4))

        def quantize(name, grouped, width):
            codes = sb.tile([P, width], U32, name=name + "_codes", align_bytes=64)
            scales = sb.tile([P, width], U8, name=name + "_scales", align_bytes=64)
            nc.vector.quantize_mx(out=codes[:].bitcast(FP8X4), scales=scales[:], in_=grouped[:].rearrange("p w t -> p (w t)"))
            return codes, scales

        def turn(dst, src, first, last):
            for j in range(BANK // P):
                cols = slice(j * P, (j + 1) * P)
                nc.tensor.matmul(dst[:, cols], lhsT=src[:, cols], rhs=ident[:], is_transpose=True,
                                 start=(first and j == 0), stop=(last and j == BANK // P - 1))

        k_scales = sb.tile([P, T], U8, align_bytes=64)
        nc.gpsimd.memset(k_scales[:].bitcast(I32), 0)
        q_raw = sb.tile([P, PACK, P], F32)
        nc.sync.dma_start(out=q_raw[:], in_=query.rearrange("(p j) w -> p j w", j=PACK))
        k_codes = sb.tile([P, T], U32, align_bytes=64)
        nc.sync.dma_start(out=k_codes[:].bitcast(I32), in_=keys_words[0].rearrange("p n t -> p (n t)").bitcast(I32))
        for quad in range(4):
            nc.sync.dma_start(out=k_scales[32 * quad : 32 * quad + 4, :].bitcast(I32),
                              in_=keys_scales[0, 4 * quad : 4 * quad + 4, :].bitcast(I32))
        list1 = sb.tile([P, SLOTS // 16], U16)
        nc.sync.dma_start(list1[:], offs)
        v_rows = vals.rearrange("(p j) w -> p j w", j=PACK)
        v_raw = [sb.tile([P, PACK, CHUNK], F32, name=f"v_raw{c}", tag=f"v_raw{c}") for c in range(T // CHUNK)]

        def load_vals(c):
            nc.sync.dma_start(out=v_raw[c][:], in_=v_rows[:, :, c * CHUNK : (c + 1) * CHUNK])

        load_vals(0)
        g_raw = sb.tile([P, PACK, P], F32)
        nc.sync.dma_start(out=g_raw[:], in_=gout.rearrange("(p j) w -> p j w", j=PACK))
        share_cols = sb.tile([P, PACK], F32)
        nc.sync.dma_start(out=share_cols[:], in_=share[0].rearrange("(p j) -> p j", j=PACK))
        for c in range(1, T // CHUNK):
            load_vals(c)
        list2 = sb.tile([P, SLOTS // 16], U16)
        nc.sync.dma_start(list2[:], offs2)
        fac_sb = sb.tile([P, T], F32)
        nc.sync.dma_start(out=fac_sb[:], in_=fac[0].partition_broadcast(P))
        old_sb = sb.tile([P, T], F32)
        nc.sync.dma_start(out=old_sb[:], in_=old)

        ident = sb.tile([P, P], F32)
        make_identity(nc, ident[:])
        minus_one = sb.tile([P, SLOTS // 2], F32)
        nc.vector.memset(minus_one[:], -1.0)
        minus_rf = sb.tile([P, T], F32)
        rg = sb.tile([P, T], F32)
        s1 = sb.tile([P, T], F32)
        for window in (minus_rf, rg, s1):
            nc.vector.memset(window[:], 0.0)

        q_grouped = sb.tile([P, P, PACK], BF16, align_bytes=64)
        interleave(nc.vector.tensor_copy, q_grouped, q_raw[:])
        q_codes, q_scales = quantize("q", q_grouped, P)
        a = sb.tile([P, T], F32)
        half_max = sb.tile([P, T // BANK], F32)
        a_banks = [bank(f"a{h}") for h in range(T // BANK)]
        for h, cols in enumerate(halves):
            acc = a_banks[h]
            nc.tensor.matmul_mx(out=acc[:], lhsT=q_codes[:].bitcast(FP8X4), lhsT_scale=q_scales[:],
                                rhs=k_codes[:, cols].bitcast(FP8X4), rhs_scale=k_scales[:, cols], start=True, stop=True)
            nc.vector.tensor_scalar(out=a[:, cols], in0=acc[:], scalar1=1.0, scalar2=None, op0=ALU.mult, op1=ALU.max,
                                    accum_out=half_max[:, h : h + 1])
        minus_max = sb.tile([P, 1], F32)
        nc.vector.tensor_reduce(out=minus_max[:], in_=half_max[:], axis=AX.X, op=ALU.max, negate=True)

        def spread(tag, columns):
            acc = bank(tag)
            for j in range(PACK):
                nc.tensor.transpose(acc[:, j * P : (j + 1) * P], columns[:, j : j + 1].to_broadcast([P, P]), ident[:])
            return acc[:].rearrange("p (j n) -> p n j", j=PACK)

        def by_word(ap):
            return ap.rearrange("p (n j) -> p n j", j=PACK)

        share_bank = spread("back0", share_cols)

        v_grouped = []

        def group_vals(first, width, tag):
            grouped = sb.tile([P, width, PACK], BF16, name=f"v_grouped{first}", tag=tag, align_bytes=64)
            c, at = divmod(first, CHUNK)
            interleave(nc.scalar.copy, grouped, v_raw[c][:, :, at : at + width])
            v_grouped.append((first, width, grouped))

        group_vals(0, P, "v_grouped_first")
        g_grouped = sb.tile([P, P, PACK], BF16, align_bytes=64)
        interleave(lambda out, in_: nc.scalar.activation(out=out, in_=in_, func=ACT.Copy), g_grouped, g_raw[:])
        g_codes, g_scales = quantize("g", g_grouped, P)

        r = sb.tile([P, SLOTS], F32)
        pieces = [(slice(i * 256, (i + 1) * 256), slice(i * 16, (i + 1) * 16)) for i in range(2)]
        for i, (slots, entries) in enumerate(pieces):
            a_listed = sb.tile([P, SLOTS // 2], F32, name=f"a_listed{i}", tag=f"a_listed{i}", align_bytes=64)
            nc.vector.tensor_copy(a_listed[:], a[:].indirect(list1[:, entries]))
            nc.scalar.activation(out=r[:, slots], in_=a_listed[:], func=ACT.Exp, bias=minus_max[:])

        share_lo = sb.tile([P, SLOTS // 2], F32, name="share_lo", tag="share_lo")
        nc.scalar.copy(out=by_word(share_lo[:]), in_=share_bank[:, 0 : P // 2, :])
        group_vals(P, P, "a_listed0")
        group_vals(CHUNK, CHUNK, "a_listed1")
        for c in range(2, T // CHUNK):
            group_vals(c * CHUNK, CHUNK, f"v_grouped{c}")
        share_hi = sb.tile([P, SLOTS // 2], F32, name="share_hi", tag=f"v_raw{T // CHUNK - 1}")
        nc.scalar.copy(out=by_word(share_hi[:]), in_=share_bank[:, P // 2 : P, :])
        share_pieces = [share_lo, share_hi]
        p = sb.tile([P, T], F32, name="p", tag="v_raw2")
        z = sb.tile([P, 1], F32)
        nc.scalar.activation(out=p[:], in_=a[:], func=ACT.Exp, bias=minus_max[:], accum_out=z[:])
        z_gain = sb.tile([P, 1], F32)
        nc.scalar.mul(out=z_gain[:], in_=z[:], mul=1.0 / GAIN)

        for slots, entries in pieces:
            nc.vector.tensor_tensor(minus_rf[:].indirect(list1[:, entries]), r[:, slots], minus_one[:], ALU.mult)
        nc.vector.tensor_tensor(rg[:].indirect(list2[:, pieces[0][1]]), r[:, pieces[0][0]], share_lo[:], ALU.mult)

        c_banks = [bank(f"c{h}") for h in range(T // BANK)]
        for first, width, grouped in v_grouped:
            v_codes, v_scales = quantize(f"v{first}", grouped, width)
            h, at = divmod(first, BANK)
            nc.tensor.matmul_mx(out=c_banks[h][:, at : at + width], lhsT=g_codes[:].bitcast(FP8X4),
                                lhsT_scale=g_scales[:], rhs=v_codes[:].bitcast(FP8X4), rhs_scale=v_scales[:],
                                start=True, stop=True)
        nc.vector.tensor_tensor(rg[:].indirect(list2[:, pieces[1][1]]), r[:, pieces[1][0]], share_hi[:], ALU.mult)
        rz = sb.tile([P, 1], F32)
        nc.vector.reciprocal(out=rz[:], in_=z_gain[:])
        drg = sb.tile([P, T], F32)
        for h, cols in enumerate(halves):
            nc.vector.scalar_tensor_tensor(out=drg[:, cols], in0=c_banks[h][:], scalar=rz[:], in1=fac_sb[:, cols],
                                           op0=ALU.mult, op1=ALU.mult)

        u_first = sb.tile([P, CHUNK], F32)
        nc.gpsimd.tensor_tensor(u_first[:], drg[:, 0:CHUNK], p[:, 0:CHUNK], ALU.mult)

        w_turned = [bank(f"turned{h}") for h in range(T // BANK)]
        for i, term in enumerate((minus_rf, p, rg)):
            for h, cols in enumerate(halves):
                turn(w_turned[h], term[:, cols], i == 0, i == 2)
        w = [bank(f"back{h}") for h in range(T // BANK)]
        for h, cols in enumerate(halves):
            w_turned_sb = sb.tile([P, BANK], F32, name=f"w_turned_sb{h}", tag=f"w_turned_sb{h}")
            nc.scalar.copy(out=w_turned_sb[:], in_=w_turned[h][:])
            turn(w[h], w_turned_sb[:], True, True)

        dra_share = sb.tile([P, SLOTS], F32)
        for (slots, entries), share_piece in zip(pieces, share_pieces):
            nc.vector.tensor_tensor(dra_share[:, slots], drg[:].indirect(list2[:, entries]), share_piece[:], ALU.mult)
        u_mid = sb.tile([P, 2 * CHUNK], F32, name="u_mid", tag=f"v_raw{T // CHUNK - 1}")
        nc.gpsimd.tensor_tensor(u_mid[:], drg[:, CHUNK : 3 * CHUNK], p[:, CHUNK : 3 * CHUNK], ALU.mult)
        drf = sb.tile([P, T], F32, name="drf", tag="w_turned_sb0")
        nc.scalar.activation(out=drf[:], in_=drg[:], func=ACT.Copy, scale=-1.0)

        terms = sb.tile([P, T], F32)
        half_sum = sb.tile([P, T // BANK], F32)
        for h, cols in enumerate(halves):
            nc.vector.scalar_tensor_tensor(out=terms[:, cols], in0=w[h][:], scalar=rz[:], in1=drg[:, cols],
                                           op0=ALU.mult, op1=ALU.mult, accum_out=half_sum[:, h : h + 1])
        u_last = sb.tile([P, CHUNK], F32)
        nc.vector.tensor_tensor(u_last[:], drg[:, 3 * CHUNK : T], p[:, 3 * CHUNK : T], ALU.mult)
        dz = sb.tile([P, 1], F32)
        half_dz = sb.tile([P, T // BANK], F32)
        nc.scalar.activation(out=half_dz[:], in_=half_sum[:], func=ACT.Copy, scale=-1.0 / GAIN, accum_out=dz[:])
        dzp = sb.tile([P, T], F32)
        for cols in halves:
            nc.scalar.activation(out=dzp[:, cols], in_=p[:, cols], func=ACT.Copy, scale=dz[:])
        dr = sb.tile([P, SLOTS], F32)
        nc.vector.tensor_tensor(dr[:], drf[:].indirect(list1[:]), dra_share[:], ALU.add)
        nc.vector.tensor_tensor(s1[:].indirect(list1[:]), dr[:], r[:], ALU.mult)

        b_turned = [bank(f"a{h}") for h in range(T // BANK)]
        for h, cols in enumerate(halves):
            turn(b_turned[h], old_sb[:, cols], True, False)
        for tile_, first in ((u_first, 0), (u_mid, CHUNK), (u_last, 3 * CHUNK)):
            for j in range(tile_.shape[1] // P):
                h, at = divmod(first + j * P, BANK)
                nc.tensor.matmul(b_turned[h][:, at : at + P], lhsT=tile_[:, j * P : (j + 1) * P], rhs=ident[:],
                                 is_transpose=True, start=False, stop=False)
        for h, cols in enumerate(halves):
            turn(b_turned[h], dzp[:, cols], False, True)
        b_turned_sb = sb.tile([P, T], F32)
        b = [bank(f"c{h}") for h in range(T // BANK)]
        for h, cols in enumerate(halves):
            nc.scalar.copy(out=b_turned_sb[:, cols], in_=b_turned[h][:])
            turn(b[h], b_turned_sb[:, cols], True, True)

        result = sb.tile([P, T], F32)
        b_first = sb.tile([P, CHUNK], F32)
        nc.scalar.copy(out=b_first[:], in_=b[0][:, 0:CHUNK])
        nc.gpsimd.tensor_tensor(result[:, 0:CHUNK], b_first[:], s1[:, 0:CHUNK], ALU.add)
        nc.scalar.dma_start(out=out[:, 0:CHUNK], in_=result[:, 0:CHUNK])
        for c in range(1, T // CHUNK):
            h, part = divmod(c, BANK // CHUNK)
            cols = slice(c * CHUNK, (c + 1) * CHUNK)
            nc.vector.tensor_tensor(result[:, cols], b[h][:, part * CHUNK : (part + 1) * CHUNK], s1[:, cols], ALU.add)
            nc.sync.dma_start(out=out[:, cols], in_=result[:, cols])
